import numpy as np
import ml_dtypes


def mxq(x, axis, fmt="e4m3"):
    dtype, down = {"e4m3": (ml_dtypes.float8_e4m3fn, 7), "e5m2": (ml_dtypes.float8_e5m2, 14)}[fmt]
    v = np.moveaxis(np.asarray(x, np.float32).astype(ml_dtypes.bfloat16).astype(np.float64), axis, -1)
    blocks = v.reshape(v.shape[:-1] + (-1, 32))
    amax = np.abs(blocks).max(-1, keepdims=True)
    byte = np.maximum(np.where(amax > 0, np.frexp(amax)[1] - 1 + 127, 0) - down, 1)
    scale = np.exp2(byte - 127.0)
    codes = (blocks / scale).astype(np.float32).astype(dtype).astype(np.float64)
    return np.moveaxis((codes * scale).reshape(v.shape), -1, axis)


WIDE = False


def mx_kscale(k):
    if not WIDE:
        return np.ones(k)
    levels = np.array([10, -10, 5, -5, 0])
    if k % 512:
        return np.exp2(np.random.permutation(np.resize(levels, k // 32))).repeat(32)
    a = np.empty((k // 512, 16))
    for p in range(k // 512):
        a[p, :8] = np.random.permutation(np.resize(levels, 8))
        for g in range(8):
            far = levels[np.abs(levels - a[p, g]) >= 10]
            a[p, g + 8] = far[np.random.randint(len(far))]
    return np.exp2(a.ravel()).repeat(32)


def f64(x):
    return np.asarray(x).astype(np.float64)


def striped(idx):
    return np.tile(idx.reshape(-1, 16).T, (8, 1)).astype(np.uint16)


def unstriped(offs):
    return offs[:16].T.reshape(-1).astype(np.int64)


E2M1 = np.array([0.0, 0.5, 1.0, 1.5, 2.0, 3.0, 4.0, 6.0, -0.0, -0.5, -1.0, -1.5, -2.0, -3.0, -4.0, -6.0])


def pack_weight(w, fmt):
    k, n = w.shape
    w = f64(np.asarray(w, np.float32).astype(ml_dtypes.bfloat16)).reshape(k // 32, 32, n)
    amax = np.abs(w).max(1)
    if fmt == "e4m3":
        byte = np.frexp(amax)[1] - 1 + 127 - 7
    else:
        mant, ex = np.frexp(amax / 6.0)
        byte = np.where(mant > 0.5, ex, ex - 1) + 127
    byte = np.clip(np.where(amax > 0, byte, 1), 1, 254)
    scaled = (w * np.exp2(127.0 - byte)[:, None, :]).reshape(k, n).astype(np.float32)
    by_word = np.ascontiguousarray(scaled.reshape(k // 512, 128, 4, n).transpose(0, 1, 3, 2))
    if fmt == "e4m3":
        words = by_word.astype(ml_dtypes.float8_e4m3fn).view(np.uint8)
    else:
        c = by_word.astype(ml_dtypes.float4_e2m1fn).view(np.uint8) & 0xF
        words = (c[..., 0::2] | (c[..., 1::2] << 4)).reshape(k // 512, 128, 2 * n)
    return np.ascontiguousarray(words), np.ascontiguousarray(byte.astype(np.uint8).reshape(k // 512, 16, n))


def unpack_weight(words, scales, fmt):
    g, _, n = scales.shape
    words = np.ascontiguousarray(words).reshape(g, 128, n, -1)
    if fmt == "e4m3":
        vals = words.view(ml_dtypes.float8_e4m3fn).astype(np.float64)
    else:
        nib = np.empty((g, 128, n, 4), np.uint8)
        nib[..., 0::2] = words & 0xF
        nib[..., 1::2] = words >> 4
        vals = E2M1[nib]
    vals = vals * np.repeat(np.exp2(scales.astype(np.float64) - 127.0), 8, axis=1)[..., None]
    return vals.transpose(0, 1, 3, 2).reshape(g * 512, n)


K, T, E, C, N = 128, 512, 16, 128, 1536
TOP = 4


def by_expert(wq, xq):
    return np.concatenate([wq[e].T @ xq[:, e * C:(e + 1) * C] for e in range(E)], axis=1)


def setup_inputs():
    n = np.random.standard_normal
    s = mx_kscale(N)[:, None]
    deal = np.repeat(np.arange(E), C).reshape(TOP, T)[:, np.random.permutation(T)]
    deal = np.take_along_axis(deal, np.argsort(np.random.rand(TOP, T), axis=0), axis=0)
    for _ in range(8):
        s_, t_ = np.random.permutation(T).reshape(2, -1); r = np.random.randint(TOP, size=T // 2); x, y = deal[r, s_].copy(), deal[r, t_].copy()
        ok = ~((deal[:, s_] == y).any(0) | (deal[:, t_] == x).any(0)); deal[r[ok], s_[ok]] = y[ok]; deal[r[ok], t_[ok]] = x[ok]
    order = np.lexsort((np.random.rand(TOP * T), deal.reshape(-1)))
    slot_token = order % T; pos = np.empty(TOP * T, np.int64); pos[order] = np.arange(TOP * T); pos = pos.reshape(TOP, T)
    g = np.random.uniform(0.5, 1.5, (TOP, T)); g = g / g.sum(0)
    w_slot = np.empty(E * C)
    for r in range(TOP): w_slot[pos[r]] = g[r]
    dy = pack_weight(n((N, T)) * s, "e4m3")
    return {
        "dy_words": dy[0],
        "dy_scales": dy[1],
        "w": (n((E, N, K)) / np.sqrt(N) / s[None]).astype(np.float32),
        "gate": np.tile(w_slot, (K, 1)).astype(np.float32),
        "offs": striped(slot_token),
        "pos1": striped(pos[0]),
        "pos2": striped(pos[1]),
        "pos3": striped(pos[2]),
        "pos4": striped(pos[3]),
    }


def reference(dy_words, dy_scales, w, gate, offs, pos1, pos2, pos3, pos4):
    idx = unstriped(offs)
    gq = unpack_weight(dy_words, dy_scales, "e4m3")[:, idx]
    dx = f64(gate) * by_expert(mxq(f64(w), 1, "e4m3"), gq)
    return dx[:, unstriped(pos1)] + dx[:, unstriped(pos2)] + dx[:, unstriped(pos3)] + dx[:, unstriped(pos4)]

@@ -1,0 +1,172 @@
+from contextlib import ExitStack
+
+import concourse.mybir as mybir
+from concourse.masks import make_identity
+
+K, T, E, C, N = 128, 512, 16, 128, 1536
+S = E * C
+P = 128
+PACK = 4
+PASSES = N // (P * PACK)
+GROUP = 1024
+WINDOW = 1376
+FLOPS = 2 * S * N * K
+BYTES = E * N * K * 4 + N * T + N * T // 32 + S * 4 + K * T * 4 + 2 * P * (S + 4 * T) // 16
+
+F32 = mybir.dt.float32
+BF16 = mybir.dt.bfloat16
+I32 = mybir.dt.int32
+U32 = mybir.dt.uint32
+U16 = mybir.dt.uint16
+U8 = mybir.dt.uint8
+FP8X4 = mybir.dt.float8_e4m3fn_x4
+ADD = mybir.AluOpType.add
+MULT = mybir.AluOpType.mult
+RUNS = {0: (4, (1024, 512)), 4: (8, (1024, 512)), 8: (10, (512, 256)), 10: (12, (512, 256)), 12: (14, (512, 256)), 14: (15, (256, 128)), 15: (16, (128, 128, 128))}
+BANKS = [(0, 4), (4, 8), (8, 12), (12, 15), (15, 16)]
+
+
+def tile_moe_bdx_lin_none_kernel(
+    tc, dy_words, dy_scales, w, gate, offs, pos1, pos2, pos3, pos4, out
+):
+    nc = tc.nc
+    with ExitStack() as ctx:
+        keep = ctx.enter_context(tc.tile_pool(name="keep", bufs=1))
+        stream = ctx.enter_context(tc.tile_pool(name="stream", bufs=12))
+        psum = ctx.enter_context(tc.psum_pool(name="psum", bufs=8))
+
+        offs_sb = keep.tile([P, S // 16], U16, name="offs_sb")
+        pos_sb = [keep.tile([P, T // 16], U16, name="pos_sb%d" % r) for r in range(4)]
+        dy_w = keep.tile([P, (PASSES - 1) * T + WINDOW], I32, name="dy_w", align_bytes=64)
+        dy_s = keep.tile([P, WINDOW], U8, name="dy_s", align_bytes=64)
+        gate_in = keep.tile([P, 16], F32, name="gate_in")
+        gate_sb = keep.tile([P, S], F32, name="gate_sb")
+        ident = keep.tile([P, P], F32, name="ident")
+        dx = keep.tile([P, S], F32, name="dx")
+
+        nc.vector.memset(dy_s[:].bitcast(I32), 0)
+        nc.vector.memset(dy_w[:, PASSES * T :], 0)
+        make_identity(nc, ident[:])
+
+        def load_words(a):
+            at = (PASSES - 1 - a) * T
+            nc.sync.dma_start(dy_w[:, at : at + T], dy_words[a].rearrange("p t d -> p (t d)").bitcast(I32))
+
+        raw = {}
+
+        def load_w(e):
+            raw[e] = stream.tile([P, PASSES, PACK * K], F32, name="raw")
+            src = w[e].rearrange("(a p j) k -> p a (j k)", a=PASSES, j=PACK)
+            if e == E - 1:
+                for a in range(PASSES):
+                    nc.sync.dma_start(raw[e][:, a, :], src[:, a, :])
+            else:
+                nc.sync.dma_start(raw[e][:], src)
+
+        nc.scalar.dma_start(gate_in[:], gate[0].rearrange("(i j) -> i j", j=16))
+        nc.sync.dma_start(offs_sb[:], offs)
+        load_words(0)
+        load_w(0)
+        for q in range(4):
+            nc.scalar.dma_start(
+                dy_s[:].bitcast(I32)[32 * q : 32 * q + 4 * PASSES, : T // 4],
+                dy_scales.bitcast(I32)[:, 4 * q : 4 * q + 4, :],
+            )
+        load_words(1)
+        load_w(1)
+        load_words(2)
+        for e in range(2, E):
+            load_w(e)
+            if e == 8:
+                for r, pos in enumerate((pos1, pos2, pos3, pos4)):
+                    nc.sync.dma_start(pos_sb[r][:], pos)
+
+        for b in range(4):
+            spread = psum.tile([P, 4, P], F32, name="bank")
+            for jj in range(4):
+                j = 4 * b + jj
+                nc.tensor.transpose(spread[:, jj, :], gate_in[:, j : j + 1].to_broadcast([P, P]), ident[:])
+            nc.scalar.copy(
+                gate_sb[:].rearrange("p (i j) -> p i j", j=16)[:, :, 4 * b : 4 * b + 4],
+                spread[:].rearrange("p j i -> p i j"),
+            )
+
+        g_w = {}
+        g_s = {}
+
+        def gather(g):
+            cols = offs_sb[:, g * GROUP // 16 : (g + 1) * GROUP // 16]
+            for a in range(PASSES):
+                g_w[g, a] = keep.tile([P, GROUP], U32, name="g_w%d_%d" % (g, a), align_bytes=64)
+                at = (PASSES - 1 - a) * T
+                nc.vector.tensor_copy(g_w[g, a][:], dy_w[:, at : at + WINDOW].bitcast(U32).indirect(cols))
+            g_s[g] = keep.tile([P, GROUP], U8, name="g_s%d" % g, align_bytes=64)
+            nc.vector.tensor_copy(g_s[g][:], dy_s[:].indirect(cols))
+
+        codes = {}
+        scales = {}
+
+        def quantise(lo, hi, widths):
+            cols = (hi - lo) * PASSES * K
+            rounded = keep.tile([P, cols * PACK], BF16, name="rounded%d" % lo, align_bytes=64)
+            words = keep.tile([P, cols], U32, name="codes%d" % lo, align_bytes=64)
+            plane = keep.tile([P, cols], U8, name="scales%d" % lo, align_bytes=64)
+            for e in range(lo, hi):
+                at = (e - lo) * PASSES * K
+                codes[e] = words[:, at : at + PASSES * K]
+                scales[e] = plane[:, at : at + PASSES * K]
+                dst = rounded[:, at * PACK : (at + PASSES * K) * PACK].rearrange(
+                    "p (a c i t) -> p a c t i", a=PASSES, i=4, t=PACK
+                )
+                src = raw[e][:].rearrange("p a (t c i) -> p a c t i", t=PACK, i=4)
+                if e == E - 1:
+                    for a in range(PASSES):
+                        nc.scalar.copy(dst[:, a], src[:, a])
+                else:
+                    nc.scalar.copy(dst, src)
+            at = 0
+            for width in widths:
+                nc.vector.quantize_mx(
+                    out=words[:, at : at + width].bitcast(FP8X4),
+                    scales=plane[:, at : at + width],
+                    in_=rounded[:, at * PACK : (at + width) * PACK],
+                )
+                at += width
+
+        for g in range(S // GROUP):
+            gather(g)
+        for lo, hi in BANKS:
+            acc = psum.tile([P, 4, P], F32, name="bank")
+            for e in range(lo, hi):
+                if e in RUNS:
+                    quantise(e, *RUNS[e])
+                g, first = divmod(e * C, GROUP)
+                for a in range(PASSES):
+                    nc.tensor.matmul_mx(
+                        out=acc[:, e - lo, :],
+                        lhsT=codes[e][:, a * K : (a + 1) * K].bitcast(FP8X4),
+                        lhsT_scale=scales[e][:, a * K : (a + 1) * K],
+                        rhs=g_w[g, a][:, first : first + C].bitcast(FP8X4),
+                        rhs_scale=g_s[g][4 * a : P, first : first + C],
+                        start=(a == 0),
+                        stop=(a == PASSES - 1),
+                    )
+            nc.vector.tensor_tensor(
+                dx[:, lo * C : hi * C],
+                acc[:, : hi - lo, :].rearrange("p e c -> p (e c)"),
+                gate_sb[:, lo * C : hi * C],
+                MULT,
+            )
+
+        half = T // 2
+        total = {}
+        for r in range(4):
+            for h in range(2):
+                picked = dx[:].indirect(pos_sb[r][:, h * half // 16 : (h + 1) * half // 16])
+                total[r, h] = keep.tile([P, half], F32, name="total%d_%d" % (r, h))
+                if r == 0:
+                    nc.vector.tensor_copy(total[r, h][:], picked)
+                else:
+                    nc.vector.tensor_tensor(total[r, h][:], picked, total[r - 1, h][:], ADD)
+        for h in range(2):
+            nc.sync.dma_start(out[:, h * half : (h + 1) * half], total[3, h][:])

@@ -23,7 +23,8 @@ FP8X4 = mybir.dt.float8_e4m3fn_x4
 ADD = mybir.AluOpType.add
 MULT = mybir.AluOpType.mult
 RUNS = {0: (4, (1024, 512)), 4: (8, (1024, 512)), 8: (10, (512, 256)), 10: (12, (512, 256)), 12: (14, (512, 256)), 14: (15, (256, 128)), 15: (16, (128, 128, 128))}
-BANKS = [(0, 4), (4, 8), (8, 12), (12, 15), (15, 16)]
+SHARED = (14,)
+BANKS = [(0, 4), (4, 8), (8, 12), (12, 14), (14, 16)]
 
 
 def tile_moe_bdx_lin_none_kernel(
@@ -42,7 +43,6 @@ def tile_moe_bdx_lin_none_kernel(
         gate_in = keep.tile([P, 16], F32, name="gate_in")
         gate_sb = keep.tile([P, S], F32, name="gate_sb")
         ident = keep.tile([P, P], F32, name="ident")
-        dx = keep.tile([P, S], F32, name="dx")
 
         nc.vector.memset(dy_s[:].bitcast(I32), 0)
         nc.vector.memset(dy_w[:, PASSES * T :], 0)
@@ -51,6 +51,12 @@ def tile_moe_bdx_lin_none_kernel(
         def load_words(a):
             at = (PASSES - 1 - a) * T
             nc.sync.dma_start(dy_w[:, at : at + T], dy_words[a].rearrange("p t d -> p (t d)").bitcast(I32))
+
+        def load_scales(q):
+            nc.sync.dma_start(
+                dy_s[:].bitcast(I32)[32 * q : 32 * q + 4 * PASSES, : T // 4],
+                dy_scales.bitcast(I32)[:, 4 * q : 4 * q + 4, :],
+            )
 
         raw = {}
 
@@ -67,16 +73,15 @@ def tile_moe_bdx_lin_none_kernel(
         nc.sync.dma_start(offs_sb[:], offs)
         load_words(0)
         load_w(0)
-        for q in range(4):
-            nc.scalar.dma_start(
-                dy_s[:].bitcast(I32)[32 * q : 32 * q + 4 * PASSES, : T // 4],
-                dy_scales.bitcast(I32)[:, 4 * q : 4 * q + 4, :],
-            )
         load_words(1)
         load_w(1)
+        load_scales(0)
         load_words(2)
+        load_scales(1)
         for e in range(2, E):
             load_w(e)
+            if e < 4:
+                load_scales(e)
             if e == 8:
                 for r, pos in enumerate((pos1, pos2, pos3, pos4)):
                     nc.sync.dma_start(pos_sb[r][:], pos)
@@ -108,7 +113,7 @@ def tile_moe_bdx_lin_none_kernel(
 
         def quantise(lo, hi, widths):
             cols = (hi - lo) * PASSES * K
-            rounded = keep.tile([P, cols * PACK], BF16, name="rounded%d" % lo, align_bytes=64)
+            rounded = keep.tile([P, cols * PACK], BF16, name="rounded%d" % lo, tag="rounded%d" % lo, align_bytes=64)
             words = keep.tile([P, cols], U32, name="codes%d" % lo, align_bytes=64)
             plane = keep.tile([P, cols], U8, name="scales%d" % lo, align_bytes=64)
             for e in range(lo, hi):
@@ -116,12 +121,16 @@ def tile_moe_bdx_lin_none_kernel(
                 codes[e] = words[:, at : at + PASSES * K]
                 scales[e] = plane[:, at : at + PASSES * K]
                 dst = rounded[:, at * PACK : (at + PASSES * K) * PACK].rearrange(
-                    "p (a c i t) -> p a c t i", a=PASSES, i=4, t=PACK
+                    "p (a c i t) -> p a c t i", a=PASSES, i=2, t=PACK
                 )
-                src = raw[e][:].rearrange("p a (t c i) -> p a c t i", t=PACK, i=4)
+                src = raw[e][:].rearrange("p a (t c i) -> p a c t i", t=PACK, i=2)
                 if e == E - 1:
-                    for a in range(PASSES):
+                    for a in range(PASSES - 1):
                         nc.scalar.copy(dst[:, a], src[:, a])
+                    nc.vector.tensor_copy(dst[:, 2], src[:, 2])
+                elif e in SHARED:
+                    nc.scalar.copy(dst[:, :2], src[:, :2])
+                    nc.vector.tensor_copy(dst[:, 2], src[:, 2])
                 else:
                     nc.scalar.copy(dst, src)
             at = 0
@@ -135,15 +144,17 @@ def tile_moe_bdx_lin_none_kernel(
 
         for g in range(S // GROUP):
             gather(g)
-        for lo, hi in BANKS:
-            acc = psum.tile([P, 4, P], F32, name="bank")
+        acc = {}
+
+        def multiply(lo, hi):
+            acc[lo] = psum.tile([P, 4, P], F32, name="bank")
             for e in range(lo, hi):
                 if e in RUNS:
                     quantise(e, *RUNS[e])
                 g, first = divmod(e * C, GROUP)
                 for a in range(PASSES):
                     nc.tensor.matmul_mx(
-                        out=acc[:, e - lo, :],
+                        out=acc[lo][:, e - lo, :],
                         lhsT=codes[e][:, a * K : (a + 1) * K].bitcast(FP8X4),
                         lhsT_scale=scales[e][:, a * K : (a + 1) * K],
                         rhs=g_w[g, a][:, first : first + C].bitcast(FP8X4),
@@ -151,12 +162,23 @@ def tile_moe_bdx_lin_none_kernel(
                         start=(a == 0),
                         stop=(a == PASSES - 1),
                     )
+
+        def weigh(lo, hi):
             nc.vector.tensor_tensor(
                 dx[:, lo * C : hi * C],
-                acc[:, : hi - lo, :].rearrange("p e c -> p (e c)"),
+                acc[lo][:, : hi - lo, :].rearrange("p e c -> p (e c)"),
                 gate_sb[:, lo * C : hi * C],
                 MULT,
             )
+
+        for lo, hi in BANKS[:3]:
+            multiply(lo, hi)
+        dx = keep.tile([P, S], F32, name="dx", tag="rounded10", align_bytes=64)
+        for lo, hi in BANKS[:3]:
+            weigh(lo, hi)
+        for lo, hi in BANKS[3:]:
+            multiply(lo, hi)
+            weigh(lo, hi)
 
         half = T // 2
         total = {}

@@ -23,8 +23,7 @@ FP8X4 = mybir.dt.float8_e4m3fn_x4
 ADD = mybir.AluOpType.add
 MULT = mybir.AluOpType.mult
 RUNS = {0: (4, (1024, 512)), 4: (8, (1024, 512)), 8: (10, (512, 256)), 10: (12, (512, 256)), 12: (14, (512, 256)), 14: (15, (256, 128)), 15: (16, (128, 128, 128))}
-SHARED = (14,)
-BANKS = [(0, 4), (4, 8), (8, 12), (12, 14), (14, 16)]
+BANKS = [(0, 4), (4, 8), (8, 12), (12, 14), (14, 15), (15, 16)]
 
 
 def tile_moe_bdx_lin_none_kernel(
@@ -33,14 +32,14 @@ def tile_moe_bdx_lin_none_kernel(
     nc = tc.nc
     with ExitStack() as ctx:
         keep = ctx.enter_context(tc.tile_pool(name="keep", bufs=1))
-        stream = ctx.enter_context(tc.tile_pool(name="stream", bufs=12))
+        stream = ctx.enter_context(tc.tile_pool(name="stream", bufs=16))
         psum = ctx.enter_context(tc.psum_pool(name="psum", bufs=8))
 
         offs_sb = keep.tile([P, S // 16], U16, name="offs_sb")
         pos_sb = [keep.tile([P, T // 16], U16, name="pos_sb%d" % r) for r in range(4)]
         dy_w = keep.tile([P, (PASSES - 1) * T + WINDOW], I32, name="dy_w", align_bytes=64)
         dy_s = keep.tile([P, WINDOW], U8, name="dy_s", align_bytes=64)
-        gate_in = keep.tile([P, 16], F32, name="gate_in")
+        gate_in = keep.tile([P, 16], F32, name="gate_in", tag="rounded0", align_bytes=64)
         gate_sb = keep.tile([P, S], F32, name="gate_sb")
         ident = keep.tile([P, P], F32, name="ident")
 
@@ -63,7 +62,7 @@ def tile_moe_bdx_lin_none_kernel(
         def load_w(e):
             raw[e] = stream.tile([P, PASSES, PACK * K], F32, name="raw")
             src = w[e].rearrange("(a p j) k -> p a (j k)", a=PASSES, j=PACK)
-            if e == E - 1:
+            if e >= E - 2:
                 for a in range(PASSES):
                     nc.sync.dma_start(raw[e][:, a, :], src[:, a, :])
             else:
@@ -82,9 +81,8 @@ def tile_moe_bdx_lin_none_kernel(
             load_w(e)
             if e < 4:
                 load_scales(e)
-            if e == 8:
-                for r, pos in enumerate((pos1, pos2, pos3, pos4)):
-                    nc.sync.dma_start(pos_sb[r][:], pos)
+        for r, pos in enumerate((pos1, pos2, pos3, pos4)):
+            nc.sync.dma_start(pos_sb[r][:], pos)
 
         for b in range(4):
             spread = psum.tile([P, 4, P], F32, name="bank")
@@ -124,13 +122,18 @@ def tile_moe_bdx_lin_none_kernel(
                     "p (a c i t) -> p a c t i", a=PASSES, i=2, t=PACK
                 )
                 src = raw[e][:].rearrange("p a (t c i) -> p a c t i", t=PACK, i=2)
-                if e == E - 1:
-                    for a in range(PASSES - 1):
-                        nc.scalar.copy(dst[:, a], src[:, a])
-                    nc.vector.tensor_copy(dst[:, 2], src[:, 2])
-                elif e in SHARED:
+                if e == E - 3:
                     nc.scalar.copy(dst[:, :2], src[:, :2])
                     nc.vector.tensor_copy(dst[:, 2], src[:, 2])
+                elif e == E - 2:
+                    nc.scalar.copy(dst[:, 0], src[:, 0])
+                    nc.vector.tensor_copy(dst[:, 1], src[:, 1])
+                    nc.scalar.copy(dst[:, 2], src[:, 2])
+                elif e == E - 1:
+                    nc.scalar.copy(dst[:, 0], src[:, 0])
+                    nc.scalar.copy(dst[:, 1], src[:, 1])
+                    nc.scalar.copy(dst[:, 2, :24], src[:, 2, :24])
+                    nc.vector.tensor_copy(dst[:, 2, 24:], src[:, 2, 24:])
                 else:
                     nc.scalar.copy(dst, src)
             at = 0

@@ -62,11 +62,8 @@ def tile_moe_bdx_lin_none_kernel(
         def load_w(e):
             raw[e] = stream.tile([P, PASSES, PACK * K], F32, name="raw")
             src = w[e].rearrange("(a p j) k -> p a (j k)", a=PASSES, j=PACK)
-            if e >= E - 2:
-                for a in range(PASSES):
-                    nc.sync.dma_start(raw[e][:, a, :], src[:, a, :])
-            else:
-                nc.sync.dma_start(raw[e][:], src)
+            for a in range(PASSES):
+                nc.sync.dma_start(raw[e][:, a, :], src[:, a, :])
 
         nc.scalar.dma_start(gate_in[:], gate[0].rearrange("(i j) -> i j", j=16))
         nc.sync.dma_start(offs_sb[:], offs)
@@ -122,20 +119,8 @@ def tile_moe_bdx_lin_none_kernel(
                     "p (a c i t) -> p a c t i", a=PASSES, i=2, t=PACK
                 )
                 src = raw[e][:].rearrange("p a (t c i) -> p a c t i", t=PACK, i=2)
-                if e == E - 3:
-                    nc.scalar.copy(dst[:, :2], src[:, :2])
-                    nc.vector.tensor_copy(dst[:, 2], src[:, 2])
-                elif e == E - 2:
-                    nc.scalar.copy(dst[:, 0], src[:, 0])
-                    nc.vector.tensor_copy(dst[:, 1], src[:, 1])
-                    nc.scalar.copy(dst[:, 2], src[:, 2])
-                elif e == E - 1:
-                    nc.scalar.copy(dst[:, 0], src[:, 0])
-                    nc.scalar.copy(dst[:, 1], src[:, 1])
-                    nc.scalar.copy(dst[:, 2, :24], src[:, 2, :24])
-                    nc.vector.tensor_copy(dst[:, 2, 24:], src[:, 2, 24:])
-                else:
-                    nc.scalar.copy(dst, src)
+                for a in range(PASSES):
+                    nc.scalar.copy(dst[:, a], src[:, a])
             at = 0
             for width in widths:
                 nc.vector.quantize_mx(

from contextlib import ExitStack

import concourse.mybir as mybir
from concourse.masks import make_identity

K, T, E, C, N = 128, 512, 16, 128, 1536
S = E * C
P = 128
PACK = 4
PASSES = N // (P * PACK)
GROUP = 1024
WINDOW = 1376
FLOPS = 2 * S * N * K
BYTES = E * N * K * 4 + N * T + N * T // 32 + S * 4 + K * T * 4 + 2 * P * (S + 4 * T) // 16

F32 = mybir.dt.float32
BF16 = mybir.dt.bfloat16
I32 = mybir.dt.int32
U32 = mybir.dt.uint32
U16 = mybir.dt.uint16
U8 = mybir.dt.uint8
FP8X4 = mybir.dt.float8_e4m3fn_x4
ADD = mybir.AluOpType.add
MULT = mybir.AluOpType.mult
RUNS = {0: (4, (1024, 512)), 4: (8, (1024, 512)), 8: (10, (512, 256)), 10: (12, (512, 256)), 12: (14, (512, 256)), 14: (15, (256, 128)), 15: (16, (128, 128, 128))}
BANKS = [(0, 4), (4, 8), (8, 12), (12, 14), (14, 15), (15, 16)]


def tile_moe_bdx_lin_none_kernel(
    tc, dy_words, dy_scales, w, gate, offs, pos1, pos2, pos3, pos4, out
):
    nc = tc.nc
    with ExitStack() as ctx:
        keep = ctx.enter_context(tc.tile_pool(name="keep", bufs=1))
        stream = ctx.enter_context(tc.tile_pool(name="stream", bufs=16))
        psum = ctx.enter_context(tc.psum_pool(name="psum", bufs=8))

        offs_sb = keep.tile([P, S // 16], U16, name="offs_sb")
        pos_sb = [keep.tile([P, T // 16], U16, name="pos_sb%d" % r) for r in range(4)]
        dy_w = keep.tile([P, (PASSES - 1) * T + WINDOW], I32, name="dy_w", align_bytes=64)
        dy_s = keep.tile([P, WINDOW], U8, name="dy_s", align_bytes=64)
        gate_in = keep.tile([P, 16], F32, name="gate_in", tag="rounded0", align_bytes=64)
        gate_sb = keep.tile([P, S], F32, name="gate_sb")
        ident = keep.tile([P, P], F32, name="ident")

        nc.vector.memset(dy_s[:].bitcast(I32), 0)
        nc.vector.memset(dy_w[:, PASSES * T :], 0)
        make_identity(nc, ident[:])

        def load_words(a):
            at = (PASSES - 1 - a) * T
            nc.sync.dma_start(dy_w[:, at : at + T], dy_words[a].rearrange("p t d -> p (t d)").bitcast(I32))

        def load_scales(q):
            nc.sync.dma_start(
                dy_s[:].bitcast(I32)[32 * q : 32 * q + 4 * PASSES, : T // 4],
                dy_scales.bitcast(I32)[:, 4 * q : 4 * q + 4, :],
            )

        raw = {}

        def load_w(e):
            raw[e] = stream.tile([P, PASSES, PACK * K], F32, name="raw")
            src = w[e].rearrange("(a p j) k -> p a (j k)", a=PASSES, j=PACK)
            for a in range(PASSES):
                nc.sync.dma_start(raw[e][:, a, :], src[:, a, :])

        nc.scalar.dma_start(gate_in[:], gate[0].rearrange("(i j) -> i j", j=16))
        nc.sync.dma_start(offs_sb[:], offs)
        load_words(0)
        load_w(0)
        load_words(1)
        load_w(1)
        load_scales(0)
        load_words(2)
        load_scales(1)
        for e in range(2, E):
            load_w(e)
            if e < 4:
                load_scales(e)
        for r, pos in enumerate((pos1, pos2, pos3, pos4)):
            nc.sync.dma_start(pos_sb[r][:], pos)

        for b in range(4):
            spread = psum.tile([P, 4, P], F32, name="bank")
            for jj in range(4):
                j = 4 * b + jj
                nc.tensor.transpose(spread[:, jj, :], gate_in[:, j : j + 1].to_broadcast([P, P]), ident[:])
            nc.scalar.copy(
                gate_sb[:].rearrange("p (i j) -> p i j", j=16)[:, :, 4 * b : 4 * b + 4],
                spread[:].rearrange("p j i -> p i j"),
            )

        g_w = {}
        g_s = {}

        def gather(g):
            cols = offs_sb[:, g * GROUP // 16 : (g + 1) * GROUP // 16]
            for a in range(PASSES):
                g_w[g, a] = keep.tile([P, GROUP], U32, name="g_w%d_%d" % (g, a), align_bytes=64)
                at = (PASSES - 1 - a) * T
                nc.vector.tensor_copy(g_w[g, a][:], dy_w[:, at : at + WINDOW].bitcast(U32).indirect(cols))
            g_s[g] = keep.tile([P, GROUP], U8, name="g_s%d" % g, align_bytes=64)
            nc.vector.tensor_copy(g_s[g][:], dy_s[:].indirect(cols))

        codes = {}
        scales = {}

        def quantise(lo, hi, widths):
            cols = (hi - lo) * PASSES * K
            rounded = keep.tile([P, cols * PACK], BF16, name="rounded%d" % lo, tag="rounded%d" % lo, align_bytes=64)
            words = keep.tile([P, cols], U32, name="codes%d" % lo, align_bytes=64)
            plane = keep.tile([P, cols], U8, name="scales%d" % lo, align_bytes=64)
            for e in range(lo, hi):
                at = (e - lo) * PASSES * K
                codes[e] = words[:, at : at + PASSES * K]
                scales[e] = plane[:, at : at + PASSES * K]
                dst = rounded[:, at * PACK : (at + PASSES * K) * PACK].rearrange(
                    "p (a c i t) -> p a c t i", a=PASSES, i=2, t=PACK
                )
                src = raw[e][:].rearrange("p a (t c i) -> p a c t i", t=PACK, i=2)
                for a in range(PASSES):
                    nc.scalar.copy(dst[:, a], src[:, a])
            at = 0
            for width in widths:
                nc.vector.quantize_mx(
                    out=words[:, at : at + width].bitcast(FP8X4),
                    scales=plane[:, at : at + width],
                    in_=rounded[:, at * PACK : (at + width) * PACK],
                )
                at += width

        for g in range(S // GROUP):
            gather(g)
        acc = {}

        def multiply(lo, hi):
            acc[lo] = psum.tile([P, 4, P], F32, name="bank")
            for e in range(lo, hi):
                if e in RUNS:
                    quantise(e, *RUNS[e])
                g, first = divmod(e * C, GROUP)
                for a in range(PASSES):
                    nc.tensor.matmul_mx(
                        out=acc[lo][:, e - lo, :],
                        lhsT=codes[e][:, a * K : (a + 1) * K].bitcast(FP8X4),
                        lhsT_scale=scales[e][:, a * K : (a + 1) * K],
                        rhs=g_w[g, a][:, first : first + C].bitcast(FP8X4),
                        rhs_scale=g_s[g][4 * a : P, first : first + C],
                        start=(a == 0),
                        stop=(a == PASSES - 1),
                    )

        def weigh(lo, hi):
            nc.vector.tensor_tensor(
                dx[:, lo * C : hi * C],
                acc[lo][:, : hi - lo, :].rearrange("p e c -> p (e c)"),
                gate_sb[:, lo * C : hi * C],
                MULT,
            )

        for lo, hi in BANKS[:3]:
            multiply(lo, hi)
        dx = keep.tile([P, S], F32, name="dx", tag="rounded10", align_bytes=64)
        for lo, hi in BANKS[:3]:
            weigh(lo, hi)
        for lo, hi in BANKS[3:]:
            multiply(lo, hi)
            weigh(lo, hi)

        half = T // 2
        total = {}
        for r in range(4):
            for h in range(2):
                picked = dx[:].indirect(pos_sb[r][:, h * half // 16 : (h + 1) * half // 16])
                total[r, h] = keep.tile([P, half], F32, name="total%d_%d" % (r, h))
                if r == 0:
                    nc.vector.tensor_copy(total[r, h][:], picked)
                else:
                    nc.vector.tensor_tensor(total[r, h][:], picked, total[r - 1, h][:], ADD)
        for h in range(2):
            nc.sync.dma_start(out[:, h * half : (h + 1) * half], total[3, h][:])
